import numpy as np
import ml_dtypes


def mxq(x, axis, fmt="e4m3"):
    dtype, down = {"e4m3": (ml_dtypes.float8_e4m3fn, 7), "e5m2": (ml_dtypes.float8_e5m2, 14)}[fmt]
    v = np.moveaxis(np.asarray(x, np.float32).astype(ml_dtypes.bfloat16).astype(np.float64), axis, -1)
    blocks = v.reshape(v.shape[:-1] + (-1, 32))
    amax = np.abs(blocks).max(-1, keepdims=True)
    byte = np.maximum(np.where(amax > 0, np.frexp(amax)[1] - 1 + 127, 0) - down, 1)
    scale = np.exp2(byte - 127.0)
    codes = (blocks / scale).astype(np.float32).astype(dtype).astype(np.float64)
    return np.moveaxis((codes * scale).reshape(v.shape), -1, axis)


WIDE = False


def mx_kscale(k):
    if not WIDE:
        return np.ones(k)
    levels = np.array([10, -10, 5, -5, 0])
    if k % 512:
        return np.exp2(np.random.permutation(np.resize(levels, k // 32))).repeat(32)
    a = np.empty((k // 512, 16))
    for p in range(k // 512):
        a[p, :8] = np.random.permutation(np.resize(levels, 8))
        for g in range(8):
            far = levels[np.abs(levels - a[p, g]) >= 10]
            a[p, g + 8] = far[np.random.randint(len(far))]
    return np.exp2(a.ravel()).repeat(32)


def f64(x):
    return np.asarray(x).astype(np.float64)


def striped(idx):
    return np.tile(idx.reshape(-1, 16).T, (8, 1)).astype(np.uint16)


def unstriped(offs):
    return offs[:16].T.reshape(-1).astype(np.int64)


def pack_weight(w):
    k, n = w.shape
    w = f64(np.asarray(w, np.float32).astype(ml_dtypes.bfloat16)).reshape(k // 32, 32, n)
    amax = np.abs(w).max(1)
    byte = np.clip(np.where(amax > 0, np.frexp(amax)[1] - 1 + 127 - 7, 1), 1, 254)
    scaled = (w * np.exp2(127.0 - byte)[:, None, :]).reshape(k, n).astype(np.float32)
    words = np.ascontiguousarray(scaled.reshape(k // 512, 128, 4, n).transpose(0, 1, 3, 2)).astype(ml_dtypes.float8_e4m3fn).view(np.uint8)
    return words, np.ascontiguousarray(byte.astype(np.uint8).reshape(k // 512, 16, n))


def unpack_weight(words, scales):
    g, p, n, _ = words.shape
    vals = np.ascontiguousarray(words).view(ml_dtypes.float8_e4m3fn).astype(np.float64) * np.repeat(np.exp2(scales.astype(np.float64) - 127.0), 8, axis=1)[..., None]
    return vals.transpose(0, 1, 3, 2).reshape(g * 512, n)


K, T, S, N, H, W, U = 512, 1024, 512, 256, 512, 1024, 1024


def setup_inputs():
    n = np.random.standard_normal
    s = mx_kscale(K)[:, None]
    u = mx_kscale(H)
    packed_xT = pack_weight(n((K, T)) * s)
    packed_eT = pack_weight(n((K, W)) * s)
    return {
        "x_words": packed_xT[0],
        "x_scales": packed_xT[1],
        "w1": (n((K, H)) / np.sqrt(K) / s).astype(np.float32),
        "e_words": packed_eT[0],
        "e_scales": packed_eT[1],
        "w2": (n((K, H)) / np.sqrt(K) / s).astype(np.float32),
        "unit": (np.random.uniform(0.6, 1.4, (H, 1)) * u[:, None]).astype(np.float32),
        "w3": (n((H, N)) / np.sqrt(H) / u[:, None]).astype(np.float32),
        "offs": striped(np.random.permutation(T)[:S]),
        "ldr": striped(np.random.permutation(W)[:S]),
        "bo": striped(np.random.permutation(np.concatenate([np.arange(S), np.random.randint(0, S, U - S)]))),
        "ln": striped(np.random.permutation(np.concatenate([np.arange(S), np.random.randint(0, S, U - S)]))),
        "gu": striped(np.random.permutation(np.concatenate([np.arange(S), np.random.randint(0, S, U - S)]))),
    }


def reference(x_words, x_scales, w1, e_words, e_scales, w2, unit, w3, offs, ldr, bo, ln, gu):
    xq = unpack_weight(x_words, x_scales)[:, unstriped(offs)]
    y = mxq(f64(w1), 0, "e4m3").T @ xq
    yb2 = y[:, unstriped(bo)]
    e_ldr = unpack_weight(e_words, e_scales)[:, unstriped(ldr)]
    ye = mxq(f64(w2), 0, "e4m3").T @ e_ldr
    el = ye[:, unstriped(ln)]
    mt = yb2 * el
    yg2 = y[:, unstriped(gu)]
    hid = f64(unit) * (mt - yg2)
    return mxq(f64(w3), 0, "e4m3").T @ mxq(hid, 0, "e4m3")

@@ -1,0 +1,234 @@
+from contextlib import ExitStack
+
+import concourse.mybir as mybir
+
+K, T, S, N, H, U = 512, 1024, 512, 256, 512, 1024
+FLOPS = 2 * K * H * S * 2 + 2 * H * N * U
+
+F32 = mybir.dt.float32
+BF16 = mybir.dt.bfloat16
+I32 = mybir.dt.int32
+U32 = mybir.dt.uint32
+U16 = mybir.dt.uint16
+U8 = mybir.dt.uint8
+FP8X4 = mybir.dt.float8_e4m3fn_x4
+COPY = mybir.ActivationFunctionType.Copy
+MULT = mybir.AluOpType.mult
+ADD = mybir.AluOpType.add
+SUBTRACT = mybir.AluOpType.subtract
+
+P = 128
+PACK = 4
+WINDOW = S + 32
+CHUNKS = (512, 256, 256)
+W_PIECES = (256, 256)
+
+
+def tile_picked_yborrow_gua_p_kernel(
+    tc, x_words, x_scales, w1, e_words, e_scales, w2, unit, w3, offs, ldr, bo, ln, gu, out
+):
+    nc = tc.nc
+    with ExitStack() as ctx:
+        keep = ctx.enter_context(tc.tile_pool(name="keep", bufs=1))
+        psum = ctx.enter_context(tc.psum_pool(name="psum", bufs=1))
+
+        def list_tile(name, src):
+            return keep.tile(list(src.shape), U16, name=name)
+
+        offs_sb = list_tile("offs_sb", offs)
+        ldr_sb = list_tile("ldr_sb", ldr)
+        bo_sb = list_tile("bo_sb", bo)
+        ln_sb = list_tile("ln_sb", ln)
+        gu_sb = list_tile("gu_sb", gu)
+        xw = keep.tile([P, T], U32, name="xw")
+        ew = keep.tile([P, T], U32, name="ew")
+        xs = keep.tile([P, T], U8, name="xs")
+        es = keep.tile([P, T], U8, name="es")
+        unit_sb = keep.tile([P, PACK], F32, name="unit_sb")
+        w_starts = [sum(W_PIECES[:h]) for h in range(len(W_PIECES))]
+        w1_raw = [keep.tile([P, PACK, n], F32, name=f"w1_raw{h}") for h, n in enumerate(W_PIECES)]
+        w2_raw = [keep.tile([P, PACK, n], F32, name=f"w2_raw{h}") for h, n in enumerate(W_PIECES)]
+        w3_raw = keep.tile([P, PACK, N], F32, name="w3_raw")
+        w1_grouped = keep.tile([P, PACK, P, PACK], BF16, name="w1_grouped", align_bytes=64)
+        w2_grouped = keep.tile([P, PACK, P, PACK], BF16, name="w2_grouped", align_bytes=64)
+        w3_grouped = keep.tile([P, N, PACK], BF16, name="w3_grouped", align_bytes=64)
+        w3_codes = keep.tile([P, N], U32, name="w3_codes", align_bytes=64)
+        w3_bytes = keep.tile([P, N], U8, name="w3_bytes", align_bytes=64)
+        x_codes = keep.tile([P, S], U32, name="x_codes", align_bytes=64)
+        x_bytes = keep.tile([P, S], U8, name="x_bytes", align_bytes=64)
+        e_codes = keep.tile([P, S], U32, name="e_codes", align_bytes=64)
+        e_bytes = keep.tile([P, S], U8, name="e_bytes", align_bytes=64)
+        uy = [keep.tile([P, WINDOW], F32, name=f"uy{t}") for t in range(PACK)]
+        ye = [keep.tile([P, WINDOW], F32, name=f"ye{t}") for t in range(PACK)]
+        borrower = [keep.tile([P, PACK, n], F32, name=f"borrower{c}") for c, n in enumerate(CHUNKS)]
+        guarantor = [keep.tile([P, PACK, n], F32, name=f"guarantor{c}") for c, n in enumerate(CHUNKS)]
+        product = [keep.tile([P, PACK, n], F32, name=f"product{c}") for c, n in enumerate(CHUNKS)]
+        hid_codes = [keep.tile([P, n], U32, name=f"hid_codes{c}", align_bytes=64) for c, n in enumerate(CHUNKS)]
+        hid_bytes = [keep.tile([P, n], U8, name=f"hid_bytes{c}", align_bytes=64) for c, n in enumerate(CHUNKS)]
+        hid = [keep.tile([P, n, PACK], BF16, name=f"hid{c}", align_bytes=64) for c, n in enumerate(CHUNKS)]
+        starts = [sum(CHUNKS[:c]) for c in range(len(CHUNKS))]
+        V, A, G = nc.vector, nc.scalar, nc.gpsimd
+
+        def clock(name, ap, dt):
+            clk = keep.tile([P, 16], dt, name=name)
+            nc.gpsimd.tensor_copy(clk[:, 0:1], ap)
+
+        def load_words(dst, src):
+            nc.sync.dma_start(dst[:].bitcast(I32), src[0].rearrange("p n t -> p (n t)").bitcast(I32))
+
+        def load_scales(queue, dst, src):
+            for q in range(4):
+                queue.dma_start(dst[32 * q : 32 * q + 4, :].bitcast(I32), src[0, 4 * q : 4 * q + 4, :].bitcast(I32))
+
+        def load_weight(dst, w, h):
+            cols = slice(w_starts[h], w_starts[h] + W_PIECES[h])
+            nc.sync.dma_start(dst[h][:], w.rearrange("(p j) c -> p j c", j=PACK)[:, :, cols])
+
+        def load(dst, src):
+            nc.sync.dma_start(dst[:], src)
+
+        def gpsimd_cast(dst, src):
+            nc.gpsimd.tensor_scalar(dst, src, 1.0, 0.0, MULT, ADD)
+
+        def deal(copy, grouped, raw, h):
+            m0, m1 = w_starts[h] // PACK, (w_starts[h] + W_PIECES[h]) // PACK
+            copy(
+                grouped[:, :, m0:m1, :].rearrange("p t m j -> p m j t"),
+                raw[h][:].rearrange("p j (m t) -> p m j t", t=PACK),
+            )
+
+        def first_product(name, grouped, codes, bytes_, t, bank):
+            wc = keep.tile([P, P], U32, name=f"{name}_c{t}", align_bytes=64)
+            ws = keep.tile([P, P], U8, name=f"{name}_s{t}", align_bytes=64)
+            nc.vector.quantize_mx(
+                out=wc[:].bitcast(FP8X4), scales=ws[:], in_=grouped[:, t].rearrange("p m j -> p (m j)")
+            )
+            acc = psum.tile([P, S], F32, name=f"{name}_bank{t}", tag=f"bank{bank}")
+            nc.tensor.matmul_mx(
+                out=acc[:], lhsT=wc[:].bitcast(FP8X4), lhsT_scale=ws[:],
+                rhs=codes[:].bitcast(FP8X4), rhs_scale=bytes_[:], start=True, stop=True,
+            )
+            return acc
+
+        def entries(offsets, c):
+            return offsets[:, starts[c] // 16 : (starts[c] + CHUNKS[c]) // 16]
+
+        def fetch(eng, dst, window, offsets):
+            if eng is A:
+                nc.scalar.activation(dst, window[:].indirect(offsets), COPY)
+            else:
+                nc.vector.tensor_copy(dst, window[:].indirect(offsets))
+
+        def fetch_a(c, t, eng=A):
+            fetch(eng, borrower[c][:, t, :], uy[t], entries(bo_sb, c))
+
+        def fetch_g(c, t, eng=A):
+            fetch(eng, guarantor[c][:, t, :], uy[t], entries(gu_sb, c))
+
+        def fetch_b(c, t):
+            nc.vector.tensor_tensor(
+                product[c][:, t, :], ye[t][:].indirect(entries(ln_sb, c)), borrower[c][:, t, :], MULT
+            )
+
+        def evac(eng, dst, src):
+            if eng is A:
+                nc.scalar.copy(dst, src)
+            else:
+                nc.vector.tensor_copy(dst, src)
+
+        def w3_cast(copy):
+            copy(
+                w3_grouped[:].rearrange("p (c i) j -> p c j i", i=2),
+                w3_raw[:].rearrange("p j (c i) -> p c j i", i=2),
+            )
+
+        def w3_quant():
+            nc.vector.quantize_mx(
+                out=w3_codes[:].bitcast(FP8X4), scales=w3_bytes[:], in_=w3_grouped[:].rearrange("p c j -> p (c j)")
+            )
+
+        def sub(c):
+            nc.vector.tensor_tensor(
+                hid[c][:].rearrange("p (r i) t -> p r t i", i=2),
+                product[c][:].rearrange("p t (r i) -> p r t i", i=2),
+                guarantor[c][:].rearrange("p t (r i) -> p r t i", i=2),
+                SUBTRACT,
+            )
+
+        def quant(c):
+            nc.vector.quantize_mx(
+                out=hid_codes[c][:].bitcast(FP8X4), scales=hid_bytes[c][:], in_=hid[c][:].rearrange("p r t -> p (r t)")
+            )
+
+        def last(c, engs):
+            n = CHUNKS[c]
+            for mt in range(N // P):
+                bank = psum.tile([P, n], F32, name=f"out_bank{c}_{mt}", tag=f"bank{(2 * c + mt) % 8}")
+                nc.tensor.matmul_mx(
+                    out=bank[:], lhsT=w3_codes[:, mt * P : (mt + 1) * P].bitcast(FP8X4),
+                    lhsT_scale=w3_bytes[:, mt * P : (mt + 1) * P],
+                    rhs=hid_codes[c][:].bitcast(FP8X4), rhs_scale=hid_bytes[c][:], start=True, stop=True,
+                )
+                result = keep.tile([P, n], F32, name=f"result{c}_{mt}")
+                evac(engs[mt], result[:], bank[:])
+                nc.sync.dma_start(out[mt * P : (mt + 1) * P, starts[c] : starts[c] + n], result[:])
+
+        nc.gpsimd.memset(xs[:].bitcast(I32), 0)
+        nc.vector.memset(es[:].bitcast(I32), 0)
+        load(offs_sb, offs)
+        load_words(xw, x_words)
+        load_scales(nc.scalar, xs, x_scales)
+        load_weight(w1_raw, w1, 0)
+        load_weight(w1_raw, w1, 1)
+        load(ldr_sb, ldr)
+        load_scales(nc.sync, es, e_scales)
+        load(unit_sb, unit.rearrange("(p t) o -> p (t o)", t=PACK))
+        load(bo_sb, bo)
+        load_words(ew, e_words)
+        load_weight(w2_raw, w2, 0)
+        load_weight(w2_raw, w2, 1)
+        load(ln_sb, ln)
+        load(gu_sb, gu)
+        load(w3_raw, w3.rearrange("(p j) c -> p j c", j=PACK))
+        nc.vector.tensor_copy(x_bytes[:], xs[:].indirect(offs_sb[:]))
+        nc.vector.tensor_copy(x_codes[:], xw[:].indirect(offs_sb[:]))
+        deal(nc.scalar.copy, w1_grouped, w1_raw, 0)
+        deal(nc.vector.tensor_copy, w1_grouped, w1_raw, 1)
+        y_banks = [first_product("w1", w1_grouped, x_codes, x_bytes, t, t) for t in range(PACK)]
+        nc.vector.tensor_copy(e_bytes[:], es[:].indirect(ldr_sb[:]))
+        for t in range(PACK):
+            nc.scalar.activation(uy[t][:, :S], y_banks[t][:], COPY, scale=unit_sb[:, t : t + 1])
+            fetch_a(0, t)
+        nc.vector.tensor_copy(e_codes[:], ew[:].indirect(ldr_sb[:]))
+        deal(nc.vector.tensor_copy, w2_grouped, w2_raw, 0)
+        deal(nc.vector.tensor_copy, w2_grouped, w2_raw, 1)
+        e_banks = [first_product("w2", w2_grouped, e_codes, e_bytes, t, PACK + t) for t in range(PACK)]
+        for t in range(PACK):
+            evac(V, ye[t][:, :S], e_banks[t][:])
+            fetch_b(0, t)
+        for t in range(PACK):
+            fetch_a(1, t)
+        for t in range(PACK):
+            fetch_g(0, t)
+        for t in range(PACK):
+            fetch_b(1, t)
+        w3_cast(nc.vector.tensor_copy)
+        w3_quant()
+        sub(0)
+        for t in range(PACK):
+            fetch_a(2, t)
+        fetch_b(2, 0)
+        quant(0)
+        for t in range(1, PACK):
+            fetch_b(2, t)
+        for t in range(PACK):
+            fetch_g(1, t)
+        for t in range(PACK):
+            fetch_g(2, t)
+        last(0, (A, A))
+        sub(1)
+        quant(1)
+        sub(2)
+        quant(2)
+        last(1, (A, A))
+        last(2, (A, V))

@@ -60,9 +60,13 @@ def tile_picked_yborrow_gua_p_kernel(
         e_bytes = keep.tile([P, S], U8, name="e_bytes", align_bytes=64)
         uy = [keep.tile([P, WINDOW], F32, name=f"uy{t}") for t in range(PACK)]
         ye = [keep.tile([P, WINDOW], F32, name=f"ye{t}") for t in range(PACK)]
-        borrower = [keep.tile([P, PACK, n], F32, name=f"borrower{c}") for c, n in enumerate(CHUNKS)]
+        borrower = [keep.tile([P, PACK, S], F32, name=f"borrower{h}") for h in range(U // S)]
         guarantor = [keep.tile([P, PACK, n], F32, name=f"guarantor{c}") for c, n in enumerate(CHUNKS)]
-        product = [keep.tile([P, PACK, n], F32, name=f"product{c}") for c, n in enumerate(CHUNKS)]
+        product = [keep.tile([P, PACK, S], F32, name=f"product{h}") for h in range(U // S)]
+        w1_codes = keep.tile([P, H], U32, name="w1_codes", align_bytes=64)
+        w1_bytes = keep.tile([P, H], U8, name="w1_bytes", align_bytes=64)
+        w2_codes = keep.tile([P, H], U32, name="w2_codes", align_bytes=64)
+        w2_bytes = keep.tile([P, H], U8, name="w2_bytes", align_bytes=64)
         hid_codes = [keep.tile([P, n], U32, name=f"hid_codes{c}", align_bytes=64) for c, n in enumerate(CHUNKS)]
         hid_bytes = [keep.tile([P, n], U8, name=f"hid_bytes{c}", align_bytes=64) for c, n in enumerate(CHUNKS)]
         hid = [keep.tile([P, n, PACK], BF16, name=f"hid{c}", align_bytes=64) for c, n in enumerate(CHUNKS)]
@@ -93,22 +97,26 @@ def tile_picked_yborrow_gua_p_kernel(
         def deal(copy, grouped, raw, h):
             m0, m1 = w_starts[h] // PACK, (w_starts[h] + W_PIECES[h]) // PACK
             copy(
-                grouped[:, :, m0:m1, :].rearrange("p t m j -> p m j t"),
-                raw[h][:].rearrange("p j (m t) -> p m j t", t=PACK),
+                grouped[:, :, m0:m1, :].rearrange("p (u v) m j -> p u m j v", v=2),
+                raw[h][:].rearrange("p j (m u v) -> p u m j v", u=2, v=2),
             )
 
-        def first_product(name, grouped, codes, bytes_, t, bank):
-            wc = keep.tile([P, P], U32, name=f"{name}_c{t}", align_bytes=64)
-            ws = keep.tile([P, P], U8, name=f"{name}_s{t}", align_bytes=64)
+        def quant_w(codes, bytes_, grouped, t0, t1):
             nc.vector.quantize_mx(
-                out=wc[:].bitcast(FP8X4), scales=ws[:], in_=grouped[:, t].rearrange("p m j -> p (m j)")
+                out=codes[:, t0 * P : t1 * P].bitcast(FP8X4), scales=bytes_[:, t0 * P : t1 * P],
+                in_=grouped[:, t0:t1].rearrange("p t m j -> p (t m j)"),
             )
+
+        def first_product(name, wc, ws, codes, bytes_, t, bank):
             acc = psum.tile([P, S], F32, name=f"{name}_bank{t}", tag=f"bank{bank}")
             nc.tensor.matmul_mx(
-                out=acc[:], lhsT=wc[:].bitcast(FP8X4), lhsT_scale=ws[:],
+                out=acc[:], lhsT=wc[:, t * P : (t + 1) * P].bitcast(FP8X4), lhsT_scale=ws[:, t * P : (t + 1) * P],
                 rhs=codes[:].bitcast(FP8X4), rhs_scale=bytes_[:], start=True, stop=True,
             )
             return acc
+
+        def half_entries(offsets, h):
+            return offsets[:, h * S // 16 : (h + 1) * S // 16]
 
         def entries(offsets, c):
             return offsets[:, starts[c] // 16 : (starts[c] + CHUNKS[c]) // 16]
@@ -120,14 +128,14 @@ def tile_picked_yborrow_gua_p_kernel(
                 nc.vector.tensor_copy(dst, window[:].indirect(offsets))
 
         def fetch_a(c, t, eng=A):
-            fetch(eng, borrower[c][:, t, :], uy[t], entries(bo_sb, c))
+            fetch(eng, borrower[c][:, t, :], uy[t], half_entries(bo_sb, c))
 
         def fetch_g(c, t, eng=A):
             fetch(eng, guarantor[c][:, t, :], uy[t], entries(gu_sb, c))
 
         def fetch_b(c, t):
             nc.vector.tensor_tensor(
-                product[c][:, t, :], ye[t][:].indirect(entries(ln_sb, c)), borrower[c][:, t, :], MULT
+                product[c][:, t, :], ye[t][:].indirect(half_entries(ln_sb, c)), borrower[c][:, t, :], MULT
             )
 
         def evac(eng, dst, src):
@@ -150,7 +158,7 @@ def tile_picked_yborrow_gua_p_kernel(
         def sub(c):
             nc.vector.tensor_tensor(
                 hid[c][:].rearrange("p (r i) t -> p r t i", i=2),
-                product[c][:].rearrange("p t (r i) -> p r t i", i=2),
+                product[starts[c] // S][:, :, starts[c] % S : starts[c] % S + CHUNKS[c]].rearrange("p t (r i) -> p r t i", i=2),
                 guarantor[c][:].rearrange("p t (r i) -> p r t i", i=2),
                 SUBTRACT,
             )
@@ -164,27 +172,29 @@ def tile_picked_yborrow_gua_p_kernel(
             n = CHUNKS[c]
             for mt in range(N // P):
                 bank = psum.tile([P, n], F32, name=f"out_bank{c}_{mt}", tag=f"bank{(2 * c + mt) % 8}")
-                nc.tensor.matmul_mx(
-                    out=bank[:], lhsT=w3_codes[:, mt * P : (mt + 1) * P].bitcast(FP8X4),
-                    lhsT_scale=w3_bytes[:, mt * P : (mt + 1) * P],
-                    rhs=hid_codes[c][:].bitcast(FP8X4), rhs_scale=hid_bytes[c][:], start=True, stop=True,
-                )
+                for n0 in range(0, n, 256 if n == 384 else n):
+                    n1 = min(n, n0 + (256 if n == 384 else n))
+                    nc.tensor.matmul_mx(
+                        out=bank[:, n0:n1], lhsT=w3_codes[:, mt * P : (mt + 1) * P].bitcast(FP8X4),
+                        lhsT_scale=w3_bytes[:, mt * P : (mt + 1) * P],
+                        rhs=hid_codes[c][:, n0:n1].bitcast(FP8X4), rhs_scale=hid_bytes[c][:, n0:n1], start=True, stop=True,
+                    )
                 result = keep.tile([P, n], F32, name=f"result{c}_{mt}")
                 evac(engs[mt], result[:], bank[:])
                 nc.sync.dma_start(out[mt * P : (mt + 1) * P, starts[c] : starts[c] + n], result[:])
 
-        nc.gpsimd.memset(xs[:].bitcast(I32), 0)
-        nc.vector.memset(es[:].bitcast(I32), 0)
         load(offs_sb, offs)
         load_words(xw, x_words)
+        nc.gpsimd.memset(xs[:].bitcast(I32), 0)
+        nc.vector.memset(es[:].bitcast(I32), 0)
         load_scales(nc.scalar, xs, x_scales)
         load_weight(w1_raw, w1, 0)
         load_weight(w1_raw, w1, 1)
-        load(ldr_sb, ldr)
-        load_scales(nc.sync, es, e_scales)
-        load(unit_sb, unit.rearrange("(p t) o -> p (t o)", t=PACK))
+        nc.gpsimd.dma_start(unit_sb[:], unit.rearrange("(p t) o -> p (t o)", t=PACK))
         load(bo_sb, bo)
         load_words(ew, e_words)
+        load(ldr_sb, ldr)
+        load_scales(nc.sync, es, e_scales)
         load_weight(w2_raw, w2, 0)
         load_weight(w2_raw, w2, 1)
         load(ln_sb, ln)
@@ -194,17 +204,23 @@ def tile_picked_yborrow_gua_p_kernel(
         nc.vector.tensor_copy(x_codes[:], xw[:].indirect(offs_sb[:]))
         deal(nc.scalar.copy, w1_grouped, w1_raw, 0)
         deal(nc.vector.tensor_copy, w1_grouped, w1_raw, 1)
-        y_banks = [first_product("w1", w1_grouped, x_codes, x_bytes, t, t) for t in range(PACK)]
-        nc.vector.tensor_copy(e_bytes[:], es[:].indirect(ldr_sb[:]))
+        quant_w(w1_codes, w1_bytes, w1_grouped, 0, 1)
+        quant_w(w1_codes, w1_bytes, w1_grouped, 1, PACK)
+        y_banks = [first_product("w1", w1_codes, w1_bytes, x_codes, x_bytes, t, t) for t in range(PACK)]
         for t in range(PACK):
             nc.scalar.activation(uy[t][:, :S], y_banks[t][:], COPY, scale=unit_sb[:, t : t + 1])
             fetch_a(0, t)
         nc.vector.tensor_copy(e_codes[:], ew[:].indirect(ldr_sb[:]))
+        nc.vector.tensor_copy(e_bytes[:], es[:].indirect(ldr_sb[:]))
         deal(nc.vector.tensor_copy, w2_grouped, w2_raw, 0)
         deal(nc.vector.tensor_copy, w2_grouped, w2_raw, 1)
-        e_banks = [first_product("w2", w2_grouped, e_codes, e_bytes, t, PACK + t) for t in range(PACK)]
+        quant_w(w2_codes, w2_bytes, w2_grouped, 0, PACK)
+        w3_cast(nc.vector.tensor_copy)
+        e_banks = [first_product("w2", w2_codes, w2_bytes, e_codes, e_bytes, t, PACK + t) for t in range(PACK)]
         for t in range(PACK):
             evac(V, ye[t][:, :S], e_banks[t][:])
+        w3_quant()
+        for t in range(PACK):
             fetch_b(0, t)
         for t in range(PACK):
             fetch_a(1, t)
@@ -212,15 +228,8 @@ def tile_picked_yborrow_gua_p_kernel(
             fetch_g(0, t)
         for t in range(PACK):
             fetch_b(1, t)
-        w3_cast(nc.vector.tensor_copy)
-        w3_quant()
         sub(0)
-        for t in range(PACK):
-            fetch_a(2, t)
-        fetch_b(2, 0)
         quant(0)
-        for t in range(1, PACK):
-            fetch_b(2, t)
         for t in range(PACK):
             fetch_g(1, t)
         for t in range(PACK):

@@ -224,10 +224,12 @@ def tile_picked_yborrow_gua_p_kernel(
             fetch_b(0, t)
         for t in range(PACK):
             fetch_a(1, t)
-        for t in range(PACK):
+        for t in range(2, PACK):
             fetch_g(0, t)
         for t in range(PACK):
             fetch_b(1, t)
+        for t in range(2):
+            fetch_g(0, t, V)
         sub(0)
         quant(0)
         for t in range(PACK):

@@ -14,14 +14,15 @@ U8 = mybir.dt.uint8
 FP8X4 = mybir.dt.float8_e4m3fn_x4
 COPY = mybir.ActivationFunctionType.Copy
 MULT = mybir.AluOpType.mult
-ADD = mybir.AluOpType.add
 SUBTRACT = mybir.AluOpType.subtract
 
 P = 128
 PACK = 4
+LANES = 16
 WINDOW = S + 32
-CHUNKS = (512, 256, 256)
-W_PIECES = (256, 256)
+HALF = U // 2
+CHUNKS = (512, 256, 128, 128)
+BANK = 512
 
 
 def tile_picked_yborrow_gua_p_kernel(
@@ -32,214 +33,176 @@ def tile_picked_yborrow_gua_p_kernel(
         keep = ctx.enter_context(tc.tile_pool(name="keep", bufs=1))
         psum = ctx.enter_context(tc.psum_pool(name="psum", bufs=1))
 
-        def list_tile(name, src):
-            return keep.tile(list(src.shape), U16, name=name)
+        def mx_tiles(name, width):
+            codes = keep.tile([P, width], U32, name=name + "_codes", align_bytes=64)
+            scales = keep.tile([P, width], U8, name=name + "_scales", align_bytes=64)
+            return codes, scales
 
-        offs_sb = list_tile("offs_sb", offs)
-        ldr_sb = list_tile("ldr_sb", ldr)
-        bo_sb = list_tile("bo_sb", bo)
-        ln_sb = list_tile("ln_sb", ln)
-        gu_sb = list_tile("gu_sb", gu)
-        xw = keep.tile([P, T], U32, name="xw")
-        ew = keep.tile([P, T], U32, name="ew")
-        xs = keep.tile([P, T], U8, name="xs")
-        es = keep.tile([P, T], U8, name="es")
-        unit_sb = keep.tile([P, PACK], F32, name="unit_sb")
-        w_starts = [sum(W_PIECES[:h]) for h in range(len(W_PIECES))]
-        w1_raw = [keep.tile([P, PACK, n], F32, name=f"w1_raw{h}") for h, n in enumerate(W_PIECES)]
-        w2_raw = [keep.tile([P, PACK, n], F32, name=f"w2_raw{h}") for h, n in enumerate(W_PIECES)]
-        w3_raw = keep.tile([P, PACK, N], F32, name="w3_raw")
-        w1_grouped = keep.tile([P, PACK, P, PACK], BF16, name="w1_grouped", align_bytes=64)
-        w2_grouped = keep.tile([P, PACK, P, PACK], BF16, name="w2_grouped", align_bytes=64)
-        w3_grouped = keep.tile([P, N, PACK], BF16, name="w3_grouped", align_bytes=64)
-        w3_codes = keep.tile([P, N], U32, name="w3_codes", align_bytes=64)
-        w3_bytes = keep.tile([P, N], U8, name="w3_bytes", align_bytes=64)
-        x_codes = keep.tile([P, S], U32, name="x_codes", align_bytes=64)
-        x_bytes = keep.tile([P, S], U8, name="x_bytes", align_bytes=64)
-        e_codes = keep.tile([P, S], U32, name="e_codes", align_bytes=64)
-        e_bytes = keep.tile([P, S], U8, name="e_bytes", align_bytes=64)
-        uy = [keep.tile([P, WINDOW], F32, name=f"uy{t}") for t in range(PACK)]
-        ye = [keep.tile([P, WINDOW], F32, name=f"ye{t}") for t in range(PACK)]
-        borrower = [keep.tile([P, PACK, S], F32, name=f"borrower{h}") for h in range(U // S)]
-        guarantor = [keep.tile([P, PACK, n], F32, name=f"guarantor{c}") for c, n in enumerate(CHUNKS)]
-        product = [keep.tile([P, PACK, S], F32, name=f"product{h}") for h in range(U // S)]
-        w1_codes = keep.tile([P, H], U32, name="w1_codes", align_bytes=64)
-        w1_bytes = keep.tile([P, H], U8, name="w1_bytes", align_bytes=64)
-        w2_codes = keep.tile([P, H], U32, name="w2_codes", align_bytes=64)
-        w2_bytes = keep.tile([P, H], U8, name="w2_bytes", align_bytes=64)
-        hid_codes = [keep.tile([P, n], U32, name=f"hid_codes{c}", align_bytes=64) for c, n in enumerate(CHUNKS)]
-        hid_bytes = [keep.tile([P, n], U8, name=f"hid_bytes{c}", align_bytes=64) for c, n in enumerate(CHUNKS)]
-        hid = [keep.tile([P, n, PACK], BF16, name=f"hid{c}", align_bytes=64) for c, n in enumerate(CHUNKS)]
-        starts = [sum(CHUNKS[:c]) for c in range(len(CHUNKS))]
-        V, A, G = nc.vector, nc.scalar, nc.gpsimd
+        def load_list(name, src):
+            tile = keep.tile(list(src.shape), U16, name=name)
+            nc.sync.dma_start(tile[:], src)
+            return tile
 
-        def clock(name, ap, dt):
-            clk = keep.tile([P, 16], dt, name=name)
-            nc.gpsimd.tensor_copy(clk[:, 0:1], ap)
+        def load_words(name, src):
+            tile = keep.tile([P, T], U32, name=name)
+            nc.sync.dma_start(tile[:].bitcast(I32), src[0].rearrange("p n t -> p (n t)").bitcast(I32))
+            return tile
 
-        def load_words(dst, src):
-            nc.sync.dma_start(dst[:].bitcast(I32), src[0].rearrange("p n t -> p (n t)").bitcast(I32))
-
-        def load_scales(queue, dst, src):
+        def load_scales(name, src, clear, queue):
+            tile = keep.tile([P, T], U8, name=name)
+            clear.memset(tile[:].bitcast(I32), 0)
             for q in range(4):
-                queue.dma_start(dst[32 * q : 32 * q + 4, :].bitcast(I32), src[0, 4 * q : 4 * q + 4, :].bitcast(I32))
+                queue.dma_start(tile[32 * q : 32 * q + 4, :].bitcast(I32), src[0, 4 * q : 4 * q + 4, :].bitcast(I32))
+            return tile
 
-        def load_weight(dst, w, h):
-            cols = slice(w_starts[h], w_starts[h] + W_PIECES[h])
-            nc.sync.dma_start(dst[h][:], w.rearrange("(p j) c -> p j c", j=PACK)[:, :, cols])
+        def load_rows(name, src, queue):
+            tile = keep.tile([P, PACK, src.shape[1]], F32, name=name)
+            queue.dma_start(tile[:], src.rearrange("(p j) c -> p j c", j=PACK))
+            return tile
 
-        def load(dst, src):
-            nc.sync.dma_start(dst[:], src)
+        offs_sb = load_list("offs_sb", offs)
+        x_table = load_words("x_table", x_words)
+        x_table_scales = load_scales("x_table_scales", x_scales, nc.gpsimd, nc.scalar)
+        w1_raw = load_rows("w1_raw", w1, nc.sync)
+        unit_sb = load_rows("unit_sb", unit, nc.gpsimd)
+        bo_sb = load_list("bo_sb", bo)
+        e_table = load_words("e_table", e_words)
+        ldr_sb = load_list("ldr_sb", ldr)
+        e_table_scales = load_scales("e_table_scales", e_scales, nc.vector, nc.sync)
+        w2_raw = load_rows("w2_raw", w2, nc.sync)
+        ln_sb = load_list("ln_sb", ln)
+        gu_sb = load_list("gu_sb", gu)
+        w3_raw = load_rows("w3_raw", w3, nc.sync)
 
-        def gpsimd_cast(dst, src):
-            nc.gpsimd.tensor_scalar(dst, src, 1.0, 0.0, MULT, ADD)
+        def quantize(operand, cols, values):
+            nc.vector.quantize_mx(out=operand[0][:, cols].bitcast(FP8X4), scales=operand[1][:, cols], in_=values)
 
-        def deal(copy, grouped, raw, h):
-            m0, m1 = w_starts[h] // PACK, (w_starts[h] + W_PIECES[h]) // PACK
-            copy(
-                grouped[:, :, m0:m1, :].rearrange("p (u v) m j -> p u m j v", v=2),
-                raw[h][:].rearrange("p j (m u v) -> p u m j v", u=2, v=2),
-            )
-
-        def quant_w(codes, bytes_, grouped, t0, t1):
-            nc.vector.quantize_mx(
-                out=codes[:, t0 * P : t1 * P].bitcast(FP8X4), scales=bytes_[:, t0 * P : t1 * P],
-                in_=grouped[:, t0:t1].rearrange("p t m j -> p (t m j)"),
-            )
-
-        def first_product(name, wc, ws, codes, bytes_, t, bank):
-            acc = psum.tile([P, S], F32, name=f"{name}_bank{t}", tag=f"bank{bank}")
+        def multiply(acc, lhs, lhs_cols, rhs):
             nc.tensor.matmul_mx(
-                out=acc[:], lhsT=wc[:, t * P : (t + 1) * P].bitcast(FP8X4), lhsT_scale=ws[:, t * P : (t + 1) * P],
-                rhs=codes[:].bitcast(FP8X4), rhs_scale=bytes_[:], start=True, stop=True,
+                out=acc, lhsT=lhs[0][:, lhs_cols].bitcast(FP8X4), lhsT_scale=lhs[1][:, lhs_cols],
+                rhs=rhs[0][:].bitcast(FP8X4), rhs_scale=rhs[1][:], start=True, stop=True,
             )
+
+        def deal(copy, name, raw, u):
+            dealt = keep.tile([P, 2, P, PACK], BF16, name=name, align_bytes=64)
+            copy(
+                dealt[:].rearrange("p v m j -> p m j v"),
+                raw[:].rearrange("p j (m u v) -> p u m j v", u=2, v=2)[:, u],
+            )
+            return dealt
+
+        def first_product(name, weights, picked, t, bank):
+            acc = psum.tile([P, S], F32, name=name, tag=f"bank{bank}")
+            multiply(acc[:], weights, slice(t * P, (t + 1) * P), picked)
             return acc
 
-        def half_entries(offsets, h):
-            return offsets[:, h * S // 16 : (h + 1) * S // 16]
+        x_picked = mx_tiles("x_picked", S)
+        nc.vector.tensor_copy(x_picked[0][:], x_table[:].indirect(offs_sb[:]))
+        nc.vector.tensor_copy(x_picked[1][:], x_table_scales[:].indirect(offs_sb[:]))
+        w1_low = deal(nc.vector.tensor_copy, "w1_low", w1_raw, 0)
+        w1_high = deal(nc.scalar.copy, "w1_high", w1_raw, 1)
+        w1_mx = mx_tiles("w1_mx", H)
+        for v in range(2):
+            quantize(w1_mx, slice(v * P, (v + 1) * P), w1_low[:, v].rearrange("p m j -> p (m j)"))
+        quantize(w1_mx, slice(2 * P, 4 * P), w1_high[:].rearrange("p v m j -> p (v m j)"))
+        y_banks = [first_product(f"y_bank{t}", w1_mx, x_picked, t, t) for t in range(PACK)]
 
-        def entries(offsets, c):
-            return offsets[:, starts[c] // 16 : (starts[c] + CHUNKS[c]) // 16]
+        uy = [keep.tile([P, WINDOW], F32, name=f"uy{t}") for t in range(PACK)]
+        ye = [keep.tile([P, WINDOW], F32, name=f"ye{t}") for t in range(PACK)]
+        borrower = [keep.tile([P, PACK, HALF], F32, name=f"borrower{h}") for h in range(2)]
+        product = [keep.tile([P, PACK, HALF], F32, name=f"product{h}") for h in range(2)]
+        guarantor = [keep.tile([P, PACK, n], F32, name=f"guarantor{c}") for c, n in enumerate(CHUNKS)]
+        hid = [keep.tile([P, n, PACK], BF16, name=f"hid{c}", align_bytes=64) for c, n in enumerate(CHUNKS)]
+        hid_mx = [mx_tiles(f"hid_mx{c}", n) for c, n in enumerate(CHUNKS)]
+        starts = [sum(CHUNKS[:c]) for c in range(len(CHUNKS))]
 
-        def fetch(eng, dst, window, offsets):
-            if eng is A:
-                nc.scalar.activation(dst, window[:].indirect(offsets), COPY)
-            else:
-                nc.vector.tensor_copy(dst, window[:].indirect(offsets))
+        def entries(offsets, start, count):
+            return offsets[:, start // LANES : (start + count) // LANES]
 
-        def fetch_a(c, t, eng=A):
-            fetch(eng, borrower[c][:, t, :], uy[t], half_entries(bo_sb, c))
+        def fetch_borrowers(h, t):
+            nc.scalar.activation(borrower[h][:, t, :], uy[t][:].indirect(entries(bo_sb, h * HALF, HALF)), COPY)
 
-        def fetch_g(c, t, eng=A):
-            fetch(eng, guarantor[c][:, t, :], uy[t], entries(gu_sb, c))
-
-        def fetch_b(c, t):
+        def times_lenders(h, t):
             nc.vector.tensor_tensor(
-                product[c][:, t, :], ye[t][:].indirect(half_entries(ln_sb, c)), borrower[c][:, t, :], MULT
+                product[h][:, t, :], ye[t][:].indirect(entries(ln_sb, h * HALF, HALF)), borrower[h][:, t, :], MULT
             )
 
-        def evac(eng, dst, src):
-            if eng is A:
-                nc.scalar.copy(dst, src)
-            else:
-                nc.vector.tensor_copy(dst, src)
+        def guarantor_window(c, t):
+            return uy[t][:].indirect(entries(gu_sb, starts[c], CHUNKS[c]))
 
-        def w3_cast(copy):
-            copy(
-                w3_grouped[:].rearrange("p (c i) j -> p c j i", i=2),
-                w3_raw[:].rearrange("p j (c i) -> p c j i", i=2),
-            )
+        def fetch_guarantors(c, t):
+            nc.scalar.activation(guarantor[c][:, t, :], guarantor_window(c, t), COPY)
 
-        def w3_quant():
-            nc.vector.quantize_mx(
-                out=w3_codes[:].bitcast(FP8X4), scales=w3_bytes[:], in_=w3_grouped[:].rearrange("p c j -> p (c j)")
-            )
-
-        def sub(c):
+        def subtract(c):
+            first = starts[c] % HALF
             nc.vector.tensor_tensor(
                 hid[c][:].rearrange("p (r i) t -> p r t i", i=2),
-                product[starts[c] // S][:, :, starts[c] % S : starts[c] % S + CHUNKS[c]].rearrange("p t (r i) -> p r t i", i=2),
+                product[starts[c] // HALF][:, :, first : first + CHUNKS[c]].rearrange("p t (r i) -> p r t i", i=2),
                 guarantor[c][:].rearrange("p t (r i) -> p r t i", i=2),
                 SUBTRACT,
             )
 
-        def quant(c):
-            nc.vector.quantize_mx(
-                out=hid_codes[c][:].bitcast(FP8X4), scales=hid_bytes[c][:], in_=hid[c][:].rearrange("p r t -> p (r t)")
-            )
+        def quantize_hid(c):
+            quantize(hid_mx[c], slice(0, CHUNKS[c]), hid[c][:].rearrange("p r t -> p (r t)"))
 
-        def last(c, engs):
+        def last_product(c, copy):
             n = CHUNKS[c]
-            for mt in range(N // P):
-                bank = psum.tile([P, n], F32, name=f"out_bank{c}_{mt}", tag=f"bank{(2 * c + mt) % 8}")
-                for n0 in range(0, n, 256 if n == 384 else n):
-                    n1 = min(n, n0 + (256 if n == 384 else n))
-                    nc.tensor.matmul_mx(
-                        out=bank[:, n0:n1], lhsT=w3_codes[:, mt * P : (mt + 1) * P].bitcast(FP8X4),
-                        lhsT_scale=w3_bytes[:, mt * P : (mt + 1) * P],
-                        rhs=hid_codes[c][:, n0:n1].bitcast(FP8X4), rhs_scale=hid_bytes[c][:, n0:n1], start=True, stop=True,
-                    )
-                result = keep.tile([P, n], F32, name=f"result{c}_{mt}")
-                evac(engs[mt], result[:], bank[:])
-                nc.sync.dma_start(out[mt * P : (mt + 1) * P, starts[c] : starts[c] + n], result[:])
+            tiles_a_bank = min(N // P, BANK // n)
+            for first in range(0, N // P, tiles_a_bank):
+                acc = psum.tile([P, tiles_a_bank, n], F32, name=f"out_bank{c}_{first}", tag=f"bank{c + first + (c > 0)}")
+                for k in range(tiles_a_bank):
+                    multiply(acc[:, k, :], w3_mx, slice((first + k) * P, (first + k + 1) * P), hid_mx[c])
+                result = keep.tile([P, tiles_a_bank, n], F32, name=f"result{c}_{first}")
+                copy(result[:], acc[:])
+                rows = out.rearrange("(k p) r -> p k r", p=P)
+                nc.sync.dma_start(rows[:, first : first + tiles_a_bank, starts[c] : starts[c] + n], result[:])
 
-        load(offs_sb, offs)
-        load_words(xw, x_words)
-        nc.gpsimd.memset(xs[:].bitcast(I32), 0)
-        nc.vector.memset(es[:].bitcast(I32), 0)
-        load_scales(nc.scalar, xs, x_scales)
-        load_weight(w1_raw, w1, 0)
-        load_weight(w1_raw, w1, 1)
-        nc.gpsimd.dma_start(unit_sb[:], unit.rearrange("(p t) o -> p (t o)", t=PACK))
-        load(bo_sb, bo)
-        load_words(ew, e_words)
-        load(ldr_sb, ldr)
-        load_scales(nc.sync, es, e_scales)
-        load_weight(w2_raw, w2, 0)
-        load_weight(w2_raw, w2, 1)
-        load(ln_sb, ln)
-        load(gu_sb, gu)
-        load(w3_raw, w3.rearrange("(p j) c -> p j c", j=PACK))
-        nc.vector.tensor_copy(x_bytes[:], xs[:].indirect(offs_sb[:]))
-        nc.vector.tensor_copy(x_codes[:], xw[:].indirect(offs_sb[:]))
-        deal(nc.scalar.copy, w1_grouped, w1_raw, 0)
-        deal(nc.vector.tensor_copy, w1_grouped, w1_raw, 1)
-        quant_w(w1_codes, w1_bytes, w1_grouped, 0, 1)
-        quant_w(w1_codes, w1_bytes, w1_grouped, 1, PACK)
-        y_banks = [first_product("w1", w1_codes, w1_bytes, x_codes, x_bytes, t, t) for t in range(PACK)]
         for t in range(PACK):
-            nc.scalar.activation(uy[t][:, :S], y_banks[t][:], COPY, scale=unit_sb[:, t : t + 1])
-            fetch_a(0, t)
-        nc.vector.tensor_copy(e_codes[:], ew[:].indirect(ldr_sb[:]))
-        nc.vector.tensor_copy(e_bytes[:], es[:].indirect(ldr_sb[:]))
-        deal(nc.vector.tensor_copy, w2_grouped, w2_raw, 0)
-        deal(nc.vector.tensor_copy, w2_grouped, w2_raw, 1)
-        quant_w(w2_codes, w2_bytes, w2_grouped, 0, PACK)
-        w3_cast(nc.vector.tensor_copy)
-        e_banks = [first_product("w2", w2_codes, w2_bytes, e_codes, e_bytes, t, PACK + t) for t in range(PACK)]
+            nc.scalar.activation(uy[t][:, :S], y_banks[t][:], COPY, scale=unit_sb[:, t, :])
+            if t > 0:
+                fetch_borrowers(0, t - 1)
+        fetch_borrowers(0, PACK - 1)
+
+        e_picked = mx_tiles("e_picked", S)
+        nc.vector.tensor_copy(e_picked[0][:], e_table[:].indirect(ldr_sb[:]))
+        nc.vector.tensor_copy(e_picked[1][:], e_table_scales[:].indirect(ldr_sb[:]))
+        w2_dealt = [deal(nc.vector.tensor_copy, f"w2_dealt{u}", w2_raw, u) for u in range(2)]
+        w2_mx = mx_tiles("w2_mx", H)
+        for u in range(2):
+            quantize(w2_mx, slice(2 * u * P, 2 * (u + 1) * P), w2_dealt[u][:].rearrange("p v m j -> p (v m j)"))
+        w3_grouped = keep.tile([P, N, PACK], BF16, name="w3_grouped", align_bytes=64)
+        nc.vector.tensor_copy(
+            w3_grouped[:].rearrange("p (c i) j -> p c j i", i=2), w3_raw[:].rearrange("p j (c i) -> p c j i", i=2)
+        )
+        e_banks = [first_product(f"e_bank{t}", w2_mx, e_picked, t, PACK + t) for t in range(PACK)]
         for t in range(PACK):
-            evac(V, ye[t][:, :S], e_banks[t][:])
-        w3_quant()
+            nc.vector.tensor_copy(ye[t][:, :S], e_banks[t][:])
+        w3_mx = mx_tiles("w3_mx", N)
+        quantize(w3_mx, slice(0, N), w3_grouped[:].rearrange("p c j -> p (c j)"))
+
         for t in range(PACK):
-            fetch_b(0, t)
+            times_lenders(0, t)
         for t in range(PACK):
-            fetch_a(1, t)
-        for t in range(2, PACK):
-            fetch_g(0, t)
+            fetch_borrowers(1, t)
         for t in range(PACK):
-            fetch_b(1, t)
-        for t in range(2):
-            fetch_g(0, t, V)
-        sub(0)
-        quant(0)
+            fetch_guarantors(0, t)
         for t in range(PACK):
-            fetch_g(1, t)
-        for t in range(PACK):
-            fetch_g(2, t)
-        last(0, (A, A))
-        sub(1)
-        quant(1)
-        sub(2)
-        quant(2)
-        last(1, (A, A))
-        last(2, (A, V))
+            times_lenders(1, t)
+        subtract(0)
+        nc.vector.tensor_copy(guarantor[1][:, PACK - 1, :], guarantor_window(1, PACK - 1))
+        quantize_hid(0)
+        for t in range(PACK - 1):
+            fetch_guarantors(1, t)
+        for c in (2, 3):
+            for t in range(PACK):
+                fetch_guarantors(c, t)
+        last_product(0, nc.scalar.copy)
+        subtract(1)
+        subtract(2)
+        quantize_hid(1)
+        subtract(3)
+        quantize_hid(2)
+        quantize_hid(3)
+        last_product(1, nc.scalar.copy)
+        last_product(2, nc.scalar.copy)
+        last_product(3, nc.vector.tensor_copy)

@@ -61,14 +61,14 @@ def tile_picked_yborrow_gua_p_kernel(
             return tile
 
         offs_sb = load_list("offs_sb", offs)
+        x_table_scales = load_scales("x_table_scales", x_scales, nc.vector, nc.sync)
         x_table = load_words("x_table", x_words)
-        x_table_scales = load_scales("x_table_scales", x_scales, nc.gpsimd, nc.scalar)
+        bo_sb = load_list("bo_sb", bo)
         w1_raw = load_rows("w1_raw", w1, nc.sync)
         unit_sb = load_rows("unit_sb", unit, nc.gpsimd)
-        bo_sb = load_list("bo_sb", bo)
         e_table = load_words("e_table", e_words)
         ldr_sb = load_list("ldr_sb", ldr)
-        e_table_scales = load_scales("e_table_scales", e_scales, nc.vector, nc.sync)
+        e_table_scales = load_scales("e_table_scales", e_scales, nc.gpsimd, nc.sync)
         w2_raw = load_rows("w2_raw", w2, nc.sync)
         ln_sb = load_list("ln_sb", ln)
         gu_sb = load_list("gu_sb", gu)
@@ -189,12 +189,10 @@ def tile_picked_yborrow_gua_p_kernel(
         for t in range(PACK):
             times_lenders(1, t)
         subtract(0)
-        nc.vector.tensor_copy(guarantor[1][:, PACK - 1, :], guarantor_window(1, PACK - 1))
+        nc.vector.tensor_copy(guarantor[2][:, PACK - 1, :], guarantor_window(2, PACK - 1))
         quantize_hid(0)
-        for t in range(PACK - 1):
-            fetch_guarantors(1, t)
-        for c in (2, 3):
-            for t in range(PACK):
+        for c in (1, 2, 3):
+            for t in range(PACK - 1 if c == 2 else PACK):
                 fetch_guarantors(c, t)
         last_product(0, nc.scalar.copy)
         subtract(1)

from contextlib import ExitStack

import concourse.mybir as mybir

K, T, S, N, H, U = 512, 1024, 512, 256, 512, 1024
FLOPS = 2 * K * H * S * 2 + 2 * H * N * U

F32 = mybir.dt.float32
BF16 = mybir.dt.bfloat16
I32 = mybir.dt.int32
U32 = mybir.dt.uint32
U16 = mybir.dt.uint16
U8 = mybir.dt.uint8
FP8X4 = mybir.dt.float8_e4m3fn_x4
COPY = mybir.ActivationFunctionType.Copy
MULT = mybir.AluOpType.mult
SUBTRACT = mybir.AluOpType.subtract

P = 128
PACK = 4
LANES = 16
WINDOW = S + 32
HALF = U // 2
CHUNKS = (512, 256, 128, 128)
BANK = 512


def tile_picked_yborrow_gua_p_kernel(
    tc, x_words, x_scales, w1, e_words, e_scales, w2, unit, w3, offs, ldr, bo, ln, gu, out
):
    nc = tc.nc
    with ExitStack() as ctx:
        keep = ctx.enter_context(tc.tile_pool(name="keep", bufs=1))
        psum = ctx.enter_context(tc.psum_pool(name="psum", bufs=1))

        def mx_tiles(name, width):
            codes = keep.tile([P, width], U32, name=name + "_codes", align_bytes=64)
            scales = keep.tile([P, width], U8, name=name + "_scales", align_bytes=64)
            return codes, scales

        def load_list(name, src):
            tile = keep.tile(list(src.shape), U16, name=name)
            nc.sync.dma_start(tile[:], src)
            return tile

        def load_words(name, src):
            tile = keep.tile([P, T], U32, name=name)
            nc.sync.dma_start(tile[:].bitcast(I32), src[0].rearrange("p n t -> p (n t)").bitcast(I32))
            return tile

        def load_scales(name, src, clear, queue):
            tile = keep.tile([P, T], U8, name=name)
            clear.memset(tile[:].bitcast(I32), 0)
            for q in range(4):
                queue.dma_start(tile[32 * q : 32 * q + 4, :].bitcast(I32), src[0, 4 * q : 4 * q + 4, :].bitcast(I32))
            return tile

        def load_rows(name, src, queue):
            tile = keep.tile([P, PACK, src.shape[1]], F32, name=name)
            queue.dma_start(tile[:], src.rearrange("(p j) c -> p j c", j=PACK))
            return tile

        offs_sb = load_list("offs_sb", offs)
        x_table_scales = load_scales("x_table_scales", x_scales, nc.vector, nc.sync)
        x_table = load_words("x_table", x_words)
        bo_sb = load_list("bo_sb", bo)
        w1_raw = load_rows("w1_raw", w1, nc.sync)
        unit_sb = load_rows("unit_sb", unit, nc.gpsimd)
        e_table = load_words("e_table", e_words)
        ldr_sb = load_list("ldr_sb", ldr)
        e_table_scales = load_scales("e_table_scales", e_scales, nc.gpsimd, nc.sync)
        w2_raw = load_rows("w2_raw", w2, nc.sync)
        ln_sb = load_list("ln_sb", ln)
        gu_sb = load_list("gu_sb", gu)
        w3_raw = load_rows("w3_raw", w3, nc.sync)

        def quantize(operand, cols, values):
            nc.vector.quantize_mx(out=operand[0][:, cols].bitcast(FP8X4), scales=operand[1][:, cols], in_=values)

        def multiply(acc, lhs, lhs_cols, rhs):
            nc.tensor.matmul_mx(
                out=acc, lhsT=lhs[0][:, lhs_cols].bitcast(FP8X4), lhsT_scale=lhs[1][:, lhs_cols],
                rhs=rhs[0][:].bitcast(FP8X4), rhs_scale=rhs[1][:], start=True, stop=True,
            )

        def deal(copy, name, raw, u):
            dealt = keep.tile([P, 2, P, PACK], BF16, name=name, align_bytes=64)
            copy(
                dealt[:].rearrange("p v m j -> p m j v"),
                raw[:].rearrange("p j (m u v) -> p u m j v", u=2, v=2)[:, u],
            )
            return dealt

        def first_product(name, weights, picked, t, bank):
            acc = psum.tile([P, S], F32, name=name, tag=f"bank{bank}")
            multiply(acc[:], weights, slice(t * P, (t + 1) * P), picked)
            return acc

        x_picked = mx_tiles("x_picked", S)
        nc.vector.tensor_copy(x_picked[0][:], x_table[:].indirect(offs_sb[:]))
        nc.vector.tensor_copy(x_picked[1][:], x_table_scales[:].indirect(offs_sb[:]))
        w1_low = deal(nc.vector.tensor_copy, "w1_low", w1_raw, 0)
        w1_high = deal(nc.scalar.copy, "w1_high", w1_raw, 1)
        w1_mx = mx_tiles("w1_mx", H)
        for v in range(2):
            quantize(w1_mx, slice(v * P, (v + 1) * P), w1_low[:, v].rearrange("p m j -> p (m j)"))
        quantize(w1_mx, slice(2 * P, 4 * P), w1_high[:].rearrange("p v m j -> p (v m j)"))
        y_banks = [first_product(f"y_bank{t}", w1_mx, x_picked, t, t) for t in range(PACK)]

        uy = [keep.tile([P, WINDOW], F32, name=f"uy{t}") for t in range(PACK)]
        ye = [keep.tile([P, WINDOW], F32, name=f"ye{t}") for t in range(PACK)]
        borrower = [keep.tile([P, PACK, HALF], F32, name=f"borrower{h}") for h in range(2)]
        product = [keep.tile([P, PACK, HALF], F32, name=f"product{h}") for h in range(2)]
        guarantor = [keep.tile([P, PACK, n], F32, name=f"guarantor{c}") for c, n in enumerate(CHUNKS)]
        hid = [keep.tile([P, n, PACK], BF16, name=f"hid{c}", align_bytes=64) for c, n in enumerate(CHUNKS)]
        hid_mx = [mx_tiles(f"hid_mx{c}", n) for c, n in enumerate(CHUNKS)]
        starts = [sum(CHUNKS[:c]) for c in range(len(CHUNKS))]

        def entries(offsets, start, count):
            return offsets[:, start // LANES : (start + count) // LANES]

        def fetch_borrowers(h, t):
            nc.scalar.activation(borrower[h][:, t, :], uy[t][:].indirect(entries(bo_sb, h * HALF, HALF)), COPY)

        def times_lenders(h, t):
            nc.vector.tensor_tensor(
                product[h][:, t, :], ye[t][:].indirect(entries(ln_sb, h * HALF, HALF)), borrower[h][:, t, :], MULT
            )

        def guarantor_window(c, t):
            return uy[t][:].indirect(entries(gu_sb, starts[c], CHUNKS[c]))

        def fetch_guarantors(c, t):
            nc.scalar.activation(guarantor[c][:, t, :], guarantor_window(c, t), COPY)

        def subtract(c):
            first = starts[c] % HALF
            nc.vector.tensor_tensor(
                hid[c][:].rearrange("p (r i) t -> p r t i", i=2),
                product[starts[c] // HALF][:, :, first : first + CHUNKS[c]].rearrange("p t (r i) -> p r t i", i=2),
                guarantor[c][:].rearrange("p t (r i) -> p r t i", i=2),
                SUBTRACT,
            )

        def quantize_hid(c):
            quantize(hid_mx[c], slice(0, CHUNKS[c]), hid[c][:].rearrange("p r t -> p (r t)"))

        def last_product(c, copy):
            n = CHUNKS[c]
            tiles_a_bank = min(N // P, BANK // n)
            for first in range(0, N // P, tiles_a_bank):
                acc = psum.tile([P, tiles_a_bank, n], F32, name=f"out_bank{c}_{first}", tag=f"bank{c + first + (c > 0)}")
                for k in range(tiles_a_bank):
                    multiply(acc[:, k, :], w3_mx, slice((first + k) * P, (first + k + 1) * P), hid_mx[c])
                result = keep.tile([P, tiles_a_bank, n], F32, name=f"result{c}_{first}")
                copy(result[:], acc[:])
                rows = out.rearrange("(k p) r -> p k r", p=P)
                nc.sync.dma_start(rows[:, first : first + tiles_a_bank, starts[c] : starts[c] + n], result[:])

        for t in range(PACK):
            nc.scalar.activation(uy[t][:, :S], y_banks[t][:], COPY, scale=unit_sb[:, t, :])
            if t > 0:
                fetch_borrowers(0, t - 1)
        fetch_borrowers(0, PACK - 1)

        e_picked = mx_tiles("e_picked", S)
        nc.vector.tensor_copy(e_picked[0][:], e_table[:].indirect(ldr_sb[:]))
        nc.vector.tensor_copy(e_picked[1][:], e_table_scales[:].indirect(ldr_sb[:]))
        w2_dealt = [deal(nc.vector.tensor_copy, f"w2_dealt{u}", w2_raw, u) for u in range(2)]
        w2_mx = mx_tiles("w2_mx", H)
        for u in range(2):
            quantize(w2_mx, slice(2 * u * P, 2 * (u + 1) * P), w2_dealt[u][:].rearrange("p v m j -> p (v m j)"))
        w3_grouped = keep.tile([P, N, PACK], BF16, name="w3_grouped", align_bytes=64)
        nc.vector.tensor_copy(
            w3_grouped[:].rearrange("p (c i) j -> p c j i", i=2), w3_raw[:].rearrange("p j (c i) -> p c j i", i=2)
        )
        e_banks = [first_product(f"e_bank{t}", w2_mx, e_picked, t, PACK + t) for t in range(PACK)]
        for t in range(PACK):
            nc.vector.tensor_copy(ye[t][:, :S], e_banks[t][:])
        w3_mx = mx_tiles("w3_mx", N)
        quantize(w3_mx, slice(0, N), w3_grouped[:].rearrange("p c j -> p (c j)"))

        for t in range(PACK):
            times_lenders(0, t)
        for t in range(PACK):
            fetch_borrowers(1, t)
        for t in range(PACK):
            fetch_guarantors(0, t)
        for t in range(PACK):
            times_lenders(1, t)
        subtract(0)
        nc.vector.tensor_copy(guarantor[2][:, PACK - 1, :], guarantor_window(2, PACK - 1))
        quantize_hid(0)
        for c in (1, 2, 3):
            for t in range(PACK - 1 if c == 2 else PACK):
                fetch_guarantors(c, t)
        last_product(0, nc.scalar.copy)
        subtract(1)
        subtract(2)
        quantize_hid(1)
        subtract(3)
        quantize_hid(2)
        quantize_hid(3)
        last_product(1, nc.scalar.copy)
        last_product(2, nc.scalar.copy)
        last_product(3, nc.vector.tensor_copy)
